import numpy as np
import ml_dtypes


def mxq(x, axis, fmt="e4m3"):
    dtype, down = {"e4m3": (ml_dtypes.float8_e4m3fn, 7), "e5m2": (ml_dtypes.float8_e5m2, 14)}[fmt]
    v = np.moveaxis(np.asarray(x, np.float32).astype(ml_dtypes.bfloat16).astype(np.float64), axis, -1)
    blocks = v.reshape(v.shape[:-1] + (-1, 32))
    amax = np.abs(blocks).max(-1, keepdims=True)
    byte = np.maximum(np.where(amax > 0, np.frexp(amax)[1] - 1 + 127, 0) - down, 1)
    scale = np.exp2(byte - 127.0)
    codes = (blocks / scale).astype(np.float32).astype(dtype).astype(np.float64)
    return np.moveaxis((codes * scale).reshape(v.shape), -1, axis)


WIDE = False


def mx_kscale(k):
    if not WIDE:
        return np.ones(k)
    levels = np.array([10, -10, 5, -5, 0])
    if k % 512:
        return np.exp2(np.random.permutation(np.resize(levels, k // 32))).repeat(32)
    a = np.empty((k // 512, 16))
    for p in range(k // 512):
        a[p, :8] = np.random.permutation(np.resize(levels, 8))
        for g in range(8):
            far = levels[np.abs(levels - a[p, g]) >= 10]
            a[p, g + 8] = far[np.random.randint(len(far))]
    return np.exp2(a.ravel()).repeat(32)


def f64(x):
    return np.asarray(x).astype(np.float64)


E2M1 = np.array([0.0, 0.5, 1.0, 1.5, 2.0, 3.0, 4.0, 6.0, -0.0, -0.5, -1.0, -1.5, -2.0, -3.0, -4.0, -6.0])


def pack_weight(w, fmt):
    k, n = w.shape
    w = f64(np.asarray(w, np.float32).astype(ml_dtypes.bfloat16)).reshape(k // 32, 32, n)
    amax = np.abs(w).max(1)
    if fmt == "e4m3":
        byte = np.frexp(amax)[1] - 1 + 127 - 7
    else:
        mant, ex = np.frexp(amax / 6.0)
        byte = np.where(mant > 0.5, ex, ex - 1) + 127
    byte = np.clip(np.where(amax > 0, byte, 1), 1, 254)
    scaled = (w * np.exp2(127.0 - byte)[:, None, :]).reshape(k, n).astype(np.float32)
    by_word = np.ascontiguousarray(scaled.reshape(k // 512, 128, 4, n).transpose(0, 1, 3, 2))
    if fmt == "e4m3":
        words = by_word.astype(ml_dtypes.float8_e4m3fn).view(np.uint8)
    else:
        c = by_word.astype(ml_dtypes.float4_e2m1fn).view(np.uint8) & 0xF
        words = (c[..., 0::2] | (c[..., 1::2] << 4)).reshape(k // 512, 128, 2 * n)
    return np.ascontiguousarray(words), np.ascontiguousarray(byte.astype(np.uint8).reshape(k // 512, 16, n))


def unpack_weight(words, scales, fmt):
    g, _, n = scales.shape
    words = np.ascontiguousarray(words).reshape(g, 128, n, -1)
    if fmt == "e4m3":
        vals = words.view(ml_dtypes.float8_e4m3fn).astype(np.float64)
    else:
        nib = np.empty((g, 128, n, 4), np.uint8)
        nib[..., 0::2] = words & 0xF
        nib[..., 1::2] = words >> 4
        vals = E2M1[nib]
    vals = vals * np.repeat(np.exp2(scales.astype(np.float64) - 127.0), 8, axis=1)[..., None]
    return vals.transpose(0, 1, 3, 2).reshape(g * 512, n)


K, M, T = 2048, 512, 1536


def setup_inputs():
    n = np.random.standard_normal
    s = mx_kscale(K)[:, None]
    p_w4 = pack_weight(n((K, M)) / np.sqrt(K) / s ** 2, "e2m1")
    p_w8 = pack_weight(n((K, M)) / np.sqrt(K) / s, "e4m3")
    return {
        "x": (n((K, T)) * s).astype(np.float32),
        "w4_words": p_w4[0],
        "w4_scales": p_w4[1],
        "w8_words": p_w8[0],
        "w8_scales": p_w8[1],
        "r": (n((1536, 512))).astype(np.float32),
    }


def reference(x, w4_words, w4_scales, w8_words, w8_scales, r):
    xa_, xb_ = mxq(f64(x) ** 2, 0, "e4m3"), mxq(f64(x), 0, "e4m3")
    w4_ = unpack_weight(w4_words, w4_scales, "e2m1")
    w8_ = unpack_weight(w8_words, w8_scales, "e4m3")
    y = xa_.T @ w4_ + xb_.T @ w8_
    return f64(r) + y

@@ -1,0 +1,171 @@
+from contextlib import ExitStack
+
+import concourse.mybir as mybir
+
+K, M, T = 2048, 512, 1536
+FLOPS = 2 * 2 * K * M * T
+
+F32 = mybir.dt.float32
+BF16 = mybir.dt.bfloat16
+I32 = mybir.dt.int32
+U32 = mybir.dt.uint32
+U8 = mybir.dt.uint8
+FP8X4 = mybir.dt.float8_e4m3fn_x4
+FP4X4 = mybir.dt.float4_e2m1fn_x4
+
+P = 128
+PACK = 4
+K_PASS = P * PACK
+PASSES = K // K_PASS
+BLOCK = 512
+TILES = BLOCK // P
+RUN = 2
+
+
+def tile_mix_feat_tm_quad_res_kernel(tc, x, w4_words, w4_scales, w8_words, w8_scales, r, out):
+    nc = tc.nc
+    units = [(a, b) for a in range(PASSES) for b in (0, 1)] + [(a, 2) for a in range(PASSES)]
+
+    with ExitStack() as ctx:
+        keep = ctx.enter_context(tc.tile_pool(name="keep", bufs=1))
+        cast = ctx.enter_context(tc.tile_pool(name="cast", bufs=3))
+        quant = ctx.enter_context(tc.tile_pool(name="quant", bufs=6))
+        psum = ctx.enter_context(tc.psum_pool(name="psum", bufs=1))
+        ctx.enter_context(tc.manual_schedule())
+
+        s8 = keep.tile([P, M], U8, name="s8", align_bytes=64)
+        s4 = keep.tile([P, PASSES, M], U8, name="s4", align_bytes=64)
+        nc.vector.memset(s8[:].bitcast(U32), 0)
+        nc.vector.memset(s4[:].bitcast(U32), 0)
+
+        raw, w8, w4, res = {}, {}, {}, {}
+
+        def load_x(u):
+            a, b = units[u]
+            raw[u] = keep.tile([P, PACK, BLOCK], F32, name="raw%d" % u)
+            src = x[a * K_PASS:(a + 1) * K_PASS, b * BLOCK:(b + 1) * BLOCK]
+            nc.sync.dma_start(out=raw[u][:], in_=src.rearrange("(p j) t -> p j t", j=PACK))
+
+        def load_w8(h):
+            w8[h] = keep.tile([P, 2, M], U32, name="w8_%d" % h, align_bytes=64)
+            src = w8_words[2 * h:2 * h + 2].rearrange("a p n i -> p a (n i)")
+            nc.sync.dma_start(out=w8[h][:].bitcast(I32), in_=src.bitcast(I32))
+
+        def load_w4(h):
+            w4[h] = keep.tile([P, 2, 2 * M], U8, name="w4_%d" % h, align_bytes=64)
+            src = w4_words[2 * h:2 * h + 2].rearrange("a p c -> p a c")
+            nc.sync.dma_start(out=w4[h][:].bitcast(I32), in_=src.bitcast(I32))
+
+        def load_s8():
+            for q in range(4):
+                nc.sync.dma_start(out=s8[32 * q:32 * q + 16, :].bitcast(I32),
+                                  in_=w8_scales[:, 4 * q:4 * q + 4, :].bitcast(I32))
+
+        def load_s4():
+            rows = w4_scales.rearrange("a (q s) n -> s q a n", s=4)
+            for s in range(4):
+                nc.sync.dma_start(out=s4[s:P:32, :, :].bitcast(I32), in_=rows[s].bitcast(I32))
+
+        def load_r(b):
+            res[b] = keep.tile([P, TILES, M], F32, name="res%d" % b)
+            nc.sync.dma_start(out=res[b][:], in_=r[b * BLOCK:(b + 1) * BLOCK, :].rearrange("(g p) n -> p g n", p=P))
+
+        def store(b, g0, g1):
+            dst = out[b * BLOCK + g0 * P:b * BLOCK + g1 * P, :]
+            nc.sync.dma_start(out=dst.rearrange("(g p) n -> p g n", p=P), in_=res[b][:, g0:g1, :])
+
+        load_x(0)
+        load_s8()
+        load_w8(0)
+        load_x(1)
+        load_w4(0)
+        load_s4()
+        load_x(2)
+        load_x(3)
+        load_w8(1)
+        load_w4(1)
+        for u in range(4, 10):
+            load_x(u)
+        load_r(0)
+        load_x(10)
+        load_x(11)
+        load_r(1)
+        load_r(2)
+
+        lin, sq, codes, acc = {}, {}, {}, {}
+
+        def walk_in(u):
+            return raw[u][:].rearrange("p j (c i) -> p c j i", i=RUN)
+
+        def walk_out(tile):
+            return tile[:].rearrange("p (c i j) -> p c j i", i=RUN, j=PACK)
+
+        def cast_unit(u):
+            sq[u] = cast.tile([P, BLOCK * PACK], BF16, name="sq", align_bytes=64)
+            nc.scalar.activation(out=walk_out(sq[u]), in_=walk_in(u), func=mybir.ActivationFunctionType.Square)
+            lin[u] = cast.tile([P, BLOCK * PACK], BF16, name="lin", align_bytes=64)
+            nc.vector.tensor_copy(out=walk_out(lin[u]), in_=walk_in(u))
+
+        def quantize(kind, u, src):
+            words = quant.tile([P, BLOCK], U32, name=kind + "_words", align_bytes=64)
+            scales = quant.tile([P, BLOCK], U8, name=kind + "_scales", align_bytes=64)
+            nc.vector.quantize_mx(out=words[:].bitcast(FP8X4), scales=scales[:], in_=src[:])
+            codes[kind, u] = (words, scales)
+
+        def open_banks(b):
+            for g in range(TILES):
+                bank = (b % 2) * TILES + g
+                acc[b, g] = psum.tile([P, M], F32, name="bank%d" % bank)
+
+        def multiply(kind, u):
+            a, b = units[u]
+            words, scales = codes[kind, u]
+            if kind == "lin":
+                rhs, rhs_scale = w8[a // 2][:, a % 2, :].bitcast(FP8X4), s8[4 * a:P, :]
+            else:
+                rhs, rhs_scale = w4[a // 2][:, a % 2, :].bitcast(FP4X4), s4[:, a, :]
+            for g in range(TILES):
+                cols = slice(g * P, (g + 1) * P)
+                nc.tensor.matmul_mx(out=acc[b, g][:], lhsT=words[:, cols].bitcast(FP8X4), lhsT_scale=scales[:, cols],
+                                    rhs=rhs, rhs_scale=rhs_scale,
+                                    start=(kind == "lin" and a == 0), stop=(kind == "sq" and a == PASSES - 1))
+
+        def add_residual(b, g):
+            nc.vector.tensor_tensor(out=res[b][:, g, :], in0=acc[b, g][:], in1=res[b][:, g, :], op=mybir.AluOpType.add)
+
+        def vector_step(u):
+            if u < len(units):
+                cast_unit(u)
+            if u > 0:
+                quantize("sq", u - 1, sq[u - 1])
+            if u < len(units):
+                quantize("lin", u, lin[u])
+
+        open_banks(0)
+        open_banks(1)
+        for u in range(9):
+            vector_step(u)
+            if u > 0:
+                multiply("sq", u - 1)
+            if u < 8:
+                multiply("lin", u)
+        vector_step(9)
+        for g in range(TILES):
+            add_residual(0, g)
+        open_banks(2)
+        multiply("lin", 8)
+        multiply("sq", 8)
+        multiply("lin", 9)
+        for u in range(10, 13):
+            vector_step(u)
+            multiply("sq", u - 1)
+            if u < 12:
+                multiply("lin", u)
+        store(0, 0, TILES)
+        for g in range(TILES):
+            add_residual(1, g)
+        store(1, 0, TILES)
+        for g in range(TILES):
+            add_residual(2, g)
+            if g % 2 == 1:
+                store(2, g - 1, g + 1)

@@ -19,7 +19,6 @@ K_PASS = P * PACK
 PASSES = K // K_PASS
 BLOCK = 512
 TILES = BLOCK // P
-RUN = 2
 
 
 def tile_mix_feat_tm_quad_res_kernel(tc, x, w4_words, w4_scales, w8_words, w8_scales, r, out):
@@ -68,11 +67,11 @@ def tile_mix_feat_tm_quad_res_kernel(tc, x, w4_words, w4_scales, w8_words, w8_sc
 
         def load_r(b):
             res[b] = keep.tile([P, TILES, M], F32, name="res%d" % b)
-            nc.sync.dma_start(out=res[b][:], in_=r[b * BLOCK:(b + 1) * BLOCK, :].rearrange("(g p) n -> p g n", p=P))
+            nc.sync.dma_start(out=res[b][:], in_=r[b * BLOCK:(b + 1) * BLOCK, :].rearrange("(p g) n -> p g n", g=TILES))
 
         def store(b, g0, g1):
-            dst = out[b * BLOCK + g0 * P:b * BLOCK + g1 * P, :]
-            nc.sync.dma_start(out=dst.rearrange("(g p) n -> p g n", p=P), in_=res[b][:, g0:g1, :])
+            dst = out[b * BLOCK:(b + 1) * BLOCK, :].rearrange("(p g) n -> p g n", g=TILES)
+            nc.sync.dma_start(out=dst[:, g0:g1, :], in_=res[b][:, g0:g1, :])
 
         load_x(0)
         load_s8()
@@ -84,21 +83,21 @@ def tile_mix_feat_tm_quad_res_kernel(tc, x, w4_words, w4_scales, w8_words, w8_sc
         load_x(3)
         load_w8(1)
         load_w4(1)
-        for u in range(4, 10):
+        for u in range(4, 9):
             load_x(u)
         load_r(0)
-        load_x(10)
-        load_x(11)
+        for u in range(9, 12):
+            load_x(u)
         load_r(1)
         load_r(2)
 
         lin, sq, codes, acc = {}, {}, {}, {}
 
         def walk_in(u):
-            return raw[u][:].rearrange("p j (c i) -> p c j i", i=RUN)
+            return raw[u][:].rearrange("p j (m g) -> p m j g", g=TILES)
 
         def walk_out(tile):
-            return tile[:].rearrange("p (c i j) -> p c j i", i=RUN, j=PACK)
+            return tile[:].rearrange("p (g m j) -> p m j g", g=TILES, j=PACK)
 
         def cast_unit(u):
             sq[u] = cast.tile([P, BLOCK * PACK], BF16, name="sq", align_bytes=64)
@@ -149,21 +148,19 @@ def tile_mix_feat_tm_quad_res_kernel(tc, x, w4_words, w4_scales, w8_words, w8_sc
                 multiply("sq", u - 1)
             if u < 8:
                 multiply("lin", u)
-        vector_step(9)
         for g in range(TILES):
             add_residual(0, g)
         open_banks(2)
         multiply("lin", 8)
-        multiply("sq", 8)
-        multiply("lin", 9)
-        for u in range(10, 13):
+        for u in range(9, 12):
             vector_step(u)
             multiply("sq", u - 1)
-            if u < 12:
-                multiply("lin", u)
-        store(0, 0, TILES)
+            multiply("lin", u)
         for g in range(TILES):
             add_residual(1, g)
+        vector_step(12)
+        multiply("sq", 11)
+        store(0, 0, TILES)
         store(1, 0, TILES)
         for g in range(TILES):
             add_residual(2, g)

@@ -17,18 +17,32 @@ P = 128
 PACK = 4
 K_PASS = P * PACK
 PASSES = K // K_PASS
-BLOCK = 512
-TILES = BLOCK // P
+GROUP = 512
+BANKS = GROUP // P
+QUADRANT = 32
+SCALE_ROWS = 4
+LATE = 2
+W_PASSES = 2
+SCALAR_SHARE = 32
+CAST_BUFS = 3
+CODE_BUFS = 6
 
 
 def tile_mix_feat_tm_quad_res_kernel(tc, x, w4_words, w4_scales, w8_words, w8_scales, r, out):
     nc = tc.nc
-    units = [(a, b) for a in range(PASSES) for b in (0, 1)] + [(a, 2) for a in range(PASSES)]
+
+    first_pass = [(0, b) for b in range(T // GROUP)]
+    early_rest = [(a, b) for a in range(1, PASSES) for b in range(LATE)]
+    late_rest = [(a, LATE) for a in range(1, PASSES)]
+    units = first_pass + early_rest + late_rest
+    held = units.index((0, LATE))
+    first_late = units.index((1, LATE))
+    last = len(units) - 1
 
     with ExitStack() as ctx:
         keep = ctx.enter_context(tc.tile_pool(name="keep", bufs=1))
-        cast = ctx.enter_context(tc.tile_pool(name="cast", bufs=3))
-        quant = ctx.enter_context(tc.tile_pool(name="quant", bufs=6))
+        cast = ctx.enter_context(tc.tile_pool(name="cast", bufs=CAST_BUFS))
+        quant = ctx.enter_context(tc.tile_pool(name="quant", bufs=CODE_BUFS))
         psum = ctx.enter_context(tc.psum_pool(name="psum", bufs=1))
         ctx.enter_context(tc.manual_schedule())
 
@@ -39,130 +53,139 @@ def tile_mix_feat_tm_quad_res_kernel(tc, x, w4_words, w4_scales, w8_words, w8_sc
 
         raw, w8, w4, res = {}, {}, {}, {}
 
-        def load_x(u):
-            a, b = units[u]
-            raw[u] = keep.tile([P, PACK, BLOCK], F32, name="raw%d" % u)
-            src = x[a * K_PASS:(a + 1) * K_PASS, b * BLOCK:(b + 1) * BLOCK]
-            nc.sync.dma_start(out=raw[u][:], in_=src.rearrange("(p j) t -> p j t", j=PACK))
+        def load_x(a, b, groups=1):
+            rows = keep.tile([P, PACK, groups * GROUP], F32, name="raw%d" % units.index((a, b)))
+            src = x[a * K_PASS:(a + 1) * K_PASS, b * GROUP:(b + groups) * GROUP]
+            nc.sync.dma_start(out=rows[:], in_=src.rearrange("(p j) t -> p j t", j=PACK))
+            for c in range(groups):
+                raw[units.index((a, b + c))] = rows[:, :, c * GROUP:(c + 1) * GROUP]
 
         def load_w8(h):
-            w8[h] = keep.tile([P, 2, M], U32, name="w8_%d" % h, align_bytes=64)
-            src = w8_words[2 * h:2 * h + 2].rearrange("a p n i -> p a (n i)")
+            w8[h] = keep.tile([P, W_PASSES, M], U32, name="w8_%d" % h, align_bytes=64)
+            src = w8_words[W_PASSES * h:W_PASSES * (h + 1)].rearrange("a p n j -> p a (n j)")
             nc.sync.dma_start(out=w8[h][:].bitcast(I32), in_=src.bitcast(I32))
 
         def load_w4(h):
-            w4[h] = keep.tile([P, 2, 2 * M], U8, name="w4_%d" % h, align_bytes=64)
-            src = w4_words[2 * h:2 * h + 2].rearrange("a p c -> p a c")
+            w4[h] = keep.tile([P, W_PASSES, 2 * M], U8, name="w4_%d" % h, align_bytes=64)
+            src = w4_words[W_PASSES * h:W_PASSES * (h + 1)].rearrange("a p c -> p a c")
             nc.sync.dma_start(out=w4[h][:].bitcast(I32), in_=src.bitcast(I32))
 
         def load_s8():
-            for q in range(4):
-                nc.sync.dma_start(out=s8[32 * q:32 * q + 16, :].bitcast(I32),
-                                  in_=w8_scales[:, 4 * q:4 * q + 4, :].bitcast(I32))
+            for quad in range(P // QUADRANT):
+                dst = s8[QUADRANT * quad:QUADRANT * quad + PASSES * SCALE_ROWS, :]
+                src = w8_scales[:, SCALE_ROWS * quad:SCALE_ROWS * (quad + 1), :]
+                nc.sync.dma_start(out=dst.bitcast(I32), in_=src.bitcast(I32))
 
         def load_s4():
-            rows = w4_scales.rearrange("a (q s) n -> s q a n", s=4)
-            for s in range(4):
-                nc.sync.dma_start(out=s4[s:P:32, :, :].bitcast(I32), in_=rows[s].bitcast(I32))
+            by_row = w4_scales.rearrange("a (quad s) n -> s quad a n", s=SCALE_ROWS)
+            for s in range(SCALE_ROWS):
+                nc.sync.dma_start(out=s4[s:P:QUADRANT, :, :].bitcast(I32), in_=by_row[s].bitcast(I32))
+
+        def by_bank(tensor, b):
+            return tensor[b * GROUP:(b + 1) * GROUP, :].rearrange("(m g) n -> m g n", g=BANKS)
 
         def load_r(b):
-            res[b] = keep.tile([P, TILES, M], F32, name="res%d" % b)
-            nc.sync.dma_start(out=res[b][:], in_=r[b * BLOCK:(b + 1) * BLOCK, :].rearrange("(p g) n -> p g n", g=TILES))
+            res[b] = keep.tile([P, BANKS, M], F32, name="res%d" % b)
+            nc.sync.dma_start(out=res[b][:], in_=by_bank(r, b))
 
         def store(b, g0, g1):
-            dst = out[b * BLOCK:(b + 1) * BLOCK, :].rearrange("(p g) n -> p g n", g=TILES)
-            nc.sync.dma_start(out=dst[:, g0:g1, :], in_=res[b][:, g0:g1, :])
+            nc.sync.dma_start(out=by_bank(out, b)[:, g0:g1, :], in_=res[b][:, g0:g1, :])
 
-        load_x(0)
+        load_x(0, 0, groups=T // GROUP)
         load_s8()
         load_w8(0)
-        load_x(1)
-        load_w4(0)
+        load_x(1, 0, groups=LATE)
         load_s4()
-        load_x(2)
-        load_x(3)
+        load_w4(0)
+        load_x(2, 0, groups=LATE)
         load_w8(1)
         load_w4(1)
-        for u in range(4, 9):
-            load_x(u)
+        load_x(3, 0)
+        load_x(3, 1)
+        load_x(1, LATE)
         load_r(0)
-        for u in range(9, 12):
-            load_x(u)
+        load_x(2, LATE)
+        load_x(3, LATE)
         load_r(1)
-        load_r(2)
+        load_r(LATE)
 
-        lin, sq, codes, acc = {}, {}, {}, {}
+        rounded, codes, acc = {}, {}, {}
 
-        def walk_in(u):
-            return raw[u][:].rearrange("p j (m g) -> p m j g", g=TILES)
+        def round_unit(u):
+            rounded["xb", u] = cast.tile([P, GROUP * PACK], BF16, name="lin", align_bytes=64)
+            rounded["xa", u] = cast.tile([P, GROUP * PACK], BF16, name="sq", align_bytes=64)
+            src = raw[u].rearrange("p j (m g) -> p m j g", g=BANKS)
+            xb = rounded["xb", u][:].rearrange("p (g m j) -> p m j g", g=BANKS, j=PACK)
+            xa = rounded["xa", u][:].rearrange("p (g m j) -> p m j g", g=BANKS, j=PACK)
+            share = SCALAR_SHARE if u >= first_late else 0
+            if share:
+                nc.scalar.copy(out=xb[:, :share], in_=src[:, :share])
+            nc.scalar.activation(out=xa, in_=src, func=mybir.ActivationFunctionType.Square)
+            nc.vector.tensor_copy(out=xb[:, share:], in_=src[:, share:])
 
-        def walk_out(tile):
-            return tile[:].rearrange("p (g m j) -> p m j g", g=TILES, j=PACK)
+        def quantize(operand, u):
+            pool, tag = (keep, operand + "_held") if u == held else (quant, operand)
+            words = pool.tile([P, GROUP], U32, name=tag + "_words", align_bytes=64)
+            scales = pool.tile([P, GROUP], U8, name=tag + "_scales", align_bytes=64)
+            nc.vector.quantize_mx(out=words[:].bitcast(FP8X4), scales=scales[:], in_=rounded[operand, u][:])
+            codes[operand, u] = (words, scales)
 
-        def cast_unit(u):
-            sq[u] = cast.tile([P, BLOCK * PACK], BF16, name="sq", align_bytes=64)
-            nc.scalar.activation(out=walk_out(sq[u]), in_=walk_in(u), func=mybir.ActivationFunctionType.Square)
-            lin[u] = cast.tile([P, BLOCK * PACK], BF16, name="lin", align_bytes=64)
-            nc.vector.tensor_copy(out=walk_out(lin[u]), in_=walk_in(u))
-
-        def quantize(kind, u, src):
-            words = quant.tile([P, BLOCK], U32, name=kind + "_words", align_bytes=64)
-            scales = quant.tile([P, BLOCK], U8, name=kind + "_scales", align_bytes=64)
-            nc.vector.quantize_mx(out=words[:].bitcast(FP8X4), scales=scales[:], in_=src[:])
-            codes[kind, u] = (words, scales)
+        def prepare(u):
+            round_unit(u)
+            if u > 0:
+                quantize("xa", u - 1)
+            quantize("xb", u)
 
         def open_banks(b):
-            for g in range(TILES):
-                bank = (b % 2) * TILES + g
-                acc[b, g] = psum.tile([P, M], F32, name="bank%d" % bank)
+            for g in range(BANKS):
+                acc[b, g] = psum.tile([P, M], F32, name="bank%d" % ((b % LATE) * BANKS + g))
 
-        def multiply(kind, u):
+        def multiply(operand, u, banks=range(BANKS)):
             a, b = units[u]
-            words, scales = codes[kind, u]
-            if kind == "lin":
-                rhs, rhs_scale = w8[a // 2][:, a % 2, :].bitcast(FP8X4), s8[4 * a:P, :]
+            words, scales = codes[operand, u]
+            if operand == "xb":
+                rhs, rhs_scale = w8[a // W_PASSES][:, a % W_PASSES, :].bitcast(FP8X4), s8[SCALE_ROWS * a:P, :]
             else:
-                rhs, rhs_scale = w4[a // 2][:, a % 2, :].bitcast(FP4X4), s4[:, a, :]
-            for g in range(TILES):
+                rhs, rhs_scale = w4[a // W_PASSES][:, a % W_PASSES, :].bitcast(FP4X4), s4[:, a, :]
+            for g in banks:
                 cols = slice(g * P, (g + 1) * P)
                 nc.tensor.matmul_mx(out=acc[b, g][:], lhsT=words[:, cols].bitcast(FP8X4), lhsT_scale=scales[:, cols],
                                     rhs=rhs, rhs_scale=rhs_scale,
-                                    start=(kind == "lin" and a == 0), stop=(kind == "sq" and a == PASSES - 1))
+                                    start=(operand == "xb" and a == 0), stop=(operand == "xa" and a == PASSES - 1))
 
         def add_residual(b, g):
             nc.vector.tensor_tensor(out=res[b][:, g, :], in0=acc[b, g][:], in1=res[b][:, g, :], op=mybir.AluOpType.add)
 
-        def vector_step(u):
-            if u < len(units):
-                cast_unit(u)
-            if u > 0:
-                quantize("sq", u - 1, sq[u - 1])
-            if u < len(units):
-                quantize("lin", u, lin[u])
-
         open_banks(0)
         open_banks(1)
-        for u in range(9):
-            vector_step(u)
-            if u > 0:
-                multiply("sq", u - 1)
-            if u < 8:
-                multiply("lin", u)
-        for g in range(TILES):
+        for u in range(first_late + 1):
+            prepare(u)
+            if u > 0 and u - 1 != held:
+                multiply("xa", u - 1)
+            if units[u][1] != LATE:
+                multiply("xb", u)
+
+        for g in range(BANKS):
             add_residual(0, g)
-        open_banks(2)
-        multiply("lin", 8)
-        for u in range(9, 12):
-            vector_step(u)
-            multiply("sq", u - 1)
-            multiply("lin", u)
-        for g in range(TILES):
+        open_banks(LATE)
+        multiply("xb", held)
+        multiply("xa", held)
+        multiply("xb", first_late)
+        for u in range(first_late + 1, last + 1):
+            prepare(u)
+            multiply("xa", u - 1)
+            if u < last:
+                multiply("xb", u)
+
+        for g in range(BANKS):
             add_residual(1, g)
-        vector_step(12)
-        multiply("sq", 11)
-        store(0, 0, TILES)
-        store(1, 0, TILES)
-        for g in range(TILES):
-            add_residual(2, g)
-            if g % 2 == 1:
-                store(2, g - 1, g + 1)
+        quantize("xa", last)
+
+        for g in range(BANKS):
+            multiply("xb", last, [g])
+            multiply("xa", last, [g])
+        store(0, 0, BANKS)
+        store(1, 0, BANKS)
+        for g in range(BANKS):
+            add_residual(LATE, g)
+            store(LATE, g, g + 1)

from contextlib import ExitStack

import concourse.mybir as mybir

K, M, T = 2048, 512, 1536
FLOPS = 2 * 2 * K * M * T

F32 = mybir.dt.float32
BF16 = mybir.dt.bfloat16
I32 = mybir.dt.int32
U32 = mybir.dt.uint32
U8 = mybir.dt.uint8
FP8X4 = mybir.dt.float8_e4m3fn_x4
FP4X4 = mybir.dt.float4_e2m1fn_x4

P = 128
PACK = 4
K_PASS = P * PACK
PASSES = K // K_PASS
GROUP = 512
BANKS = GROUP // P
QUADRANT = 32
SCALE_ROWS = 4
LATE = 2
W_PASSES = 2
SCALAR_SHARE = 32
CAST_BUFS = 3
CODE_BUFS = 6


def tile_mix_feat_tm_quad_res_kernel(tc, x, w4_words, w4_scales, w8_words, w8_scales, r, out):
    nc = tc.nc

    first_pass = [(0, b) for b in range(T // GROUP)]
    early_rest = [(a, b) for a in range(1, PASSES) for b in range(LATE)]
    late_rest = [(a, LATE) for a in range(1, PASSES)]
    units = first_pass + early_rest + late_rest
    held = units.index((0, LATE))
    first_late = units.index((1, LATE))
    last = len(units) - 1

    with ExitStack() as ctx:
        keep = ctx.enter_context(tc.tile_pool(name="keep", bufs=1))
        cast = ctx.enter_context(tc.tile_pool(name="cast", bufs=CAST_BUFS))
        quant = ctx.enter_context(tc.tile_pool(name="quant", bufs=CODE_BUFS))
        psum = ctx.enter_context(tc.psum_pool(name="psum", bufs=1))
        ctx.enter_context(tc.manual_schedule())

        s8 = keep.tile([P, M], U8, name="s8", align_bytes=64)
        s4 = keep.tile([P, PASSES, M], U8, name="s4", align_bytes=64)
        nc.vector.memset(s8[:].bitcast(U32), 0)
        nc.vector.memset(s4[:].bitcast(U32), 0)

        raw, w8, w4, res = {}, {}, {}, {}

        def load_x(a, b, groups=1):
            rows = keep.tile([P, PACK, groups * GROUP], F32, name="raw%d" % units.index((a, b)))
            src = x[a * K_PASS:(a + 1) * K_PASS, b * GROUP:(b + groups) * GROUP]
            nc.sync.dma_start(out=rows[:], in_=src.rearrange("(p j) t -> p j t", j=PACK))
            for c in range(groups):
                raw[units.index((a, b + c))] = rows[:, :, c * GROUP:(c + 1) * GROUP]

        def load_w8(h):
            w8[h] = keep.tile([P, W_PASSES, M], U32, name="w8_%d" % h, align_bytes=64)
            src = w8_words[W_PASSES * h:W_PASSES * (h + 1)].rearrange("a p n j -> p a (n j)")
            nc.sync.dma_start(out=w8[h][:].bitcast(I32), in_=src.bitcast(I32))

        def load_w4(h):
            w4[h] = keep.tile([P, W_PASSES, 2 * M], U8, name="w4_%d" % h, align_bytes=64)
            src = w4_words[W_PASSES * h:W_PASSES * (h + 1)].rearrange("a p c -> p a c")
            nc.sync.dma_start(out=w4[h][:].bitcast(I32), in_=src.bitcast(I32))

        def load_s8():
            for quad in range(P // QUADRANT):
                dst = s8[QUADRANT * quad:QUADRANT * quad + PASSES * SCALE_ROWS, :]
                src = w8_scales[:, SCALE_ROWS * quad:SCALE_ROWS * (quad + 1), :]
                nc.sync.dma_start(out=dst.bitcast(I32), in_=src.bitcast(I32))

        def load_s4():
            by_row = w4_scales.rearrange("a (quad s) n -> s quad a n", s=SCALE_ROWS)
            for s in range(SCALE_ROWS):
                nc.sync.dma_start(out=s4[s:P:QUADRANT, :, :].bitcast(I32), in_=by_row[s].bitcast(I32))

        def by_bank(tensor, b):
            return tensor[b * GROUP:(b + 1) * GROUP, :].rearrange("(m g) n -> m g n", g=BANKS)

        def load_r(b):
            res[b] = keep.tile([P, BANKS, M], F32, name="res%d" % b)
            nc.sync.dma_start(out=res[b][:], in_=by_bank(r, b))

        def store(b, g0, g1):
            nc.sync.dma_start(out=by_bank(out, b)[:, g0:g1, :], in_=res[b][:, g0:g1, :])

        load_x(0, 0, groups=T // GROUP)
        load_s8()
        load_w8(0)
        load_x(1, 0, groups=LATE)
        load_s4()
        load_w4(0)
        load_x(2, 0, groups=LATE)
        load_w8(1)
        load_w4(1)
        load_x(3, 0)
        load_x(3, 1)
        load_x(1, LATE)
        load_r(0)
        load_x(2, LATE)
        load_x(3, LATE)
        load_r(1)
        load_r(LATE)

        rounded, codes, acc = {}, {}, {}

        def round_unit(u):
            rounded["xb", u] = cast.tile([P, GROUP * PACK], BF16, name="lin", align_bytes=64)
            rounded["xa", u] = cast.tile([P, GROUP * PACK], BF16, name="sq", align_bytes=64)
            src = raw[u].rearrange("p j (m g) -> p m j g", g=BANKS)
            xb = rounded["xb", u][:].rearrange("p (g m j) -> p m j g", g=BANKS, j=PACK)
            xa = rounded["xa", u][:].rearrange("p (g m j) -> p m j g", g=BANKS, j=PACK)
            share = SCALAR_SHARE if u >= first_late else 0
            if share:
                nc.scalar.copy(out=xb[:, :share], in_=src[:, :share])
            nc.scalar.activation(out=xa, in_=src, func=mybir.ActivationFunctionType.Square)
            nc.vector.tensor_copy(out=xb[:, share:], in_=src[:, share:])

        def quantize(operand, u):
            pool, tag = (keep, operand + "_held") if u == held else (quant, operand)
            words = pool.tile([P, GROUP], U32, name=tag + "_words", align_bytes=64)
            scales = pool.tile([P, GROUP], U8, name=tag + "_scales", align_bytes=64)
            nc.vector.quantize_mx(out=words[:].bitcast(FP8X4), scales=scales[:], in_=rounded[operand, u][:])
            codes[operand, u] = (words, scales)

        def prepare(u):
            round_unit(u)
            if u > 0:
                quantize("xa", u - 1)
            quantize("xb", u)

        def open_banks(b):
            for g in range(BANKS):
                acc[b, g] = psum.tile([P, M], F32, name="bank%d" % ((b % LATE) * BANKS + g))

        def multiply(operand, u, banks=range(BANKS)):
            a, b = units[u]
            words, scales = codes[operand, u]
            if operand == "xb":
                rhs, rhs_scale = w8[a // W_PASSES][:, a % W_PASSES, :].bitcast(FP8X4), s8[SCALE_ROWS * a:P, :]
            else:
                rhs, rhs_scale = w4[a // W_PASSES][:, a % W_PASSES, :].bitcast(FP4X4), s4[:, a, :]
            for g in banks:
                cols = slice(g * P, (g + 1) * P)
                nc.tensor.matmul_mx(out=acc[b, g][:], lhsT=words[:, cols].bitcast(FP8X4), lhsT_scale=scales[:, cols],
                                    rhs=rhs, rhs_scale=rhs_scale,
                                    start=(operand == "xb" and a == 0), stop=(operand == "xa" and a == PASSES - 1))

        def add_residual(b, g):
            nc.vector.tensor_tensor(out=res[b][:, g, :], in0=acc[b, g][:], in1=res[b][:, g, :], op=mybir.AluOpType.add)

        open_banks(0)
        open_banks(1)
        for u in range(first_late + 1):
            prepare(u)
            if u > 0 and u - 1 != held:
                multiply("xa", u - 1)
            if units[u][1] != LATE:
                multiply("xb", u)

        for g in range(BANKS):
            add_residual(0, g)
        open_banks(LATE)
        multiply("xb", held)
        multiply("xa", held)
        multiply("xb", first_late)
        for u in range(first_late + 1, last + 1):
            prepare(u)
            multiply("xa", u - 1)
            if u < last:
                multiply("xb", u)

        for g in range(BANKS):
            add_residual(1, g)
        quantize("xa", last)

        for g in range(BANKS):
            multiply("xb", last, [g])
            multiply("xa", last, [g])
        store(0, 0, BANKS)
        store(1, 0, BANKS)
        for g in range(BANKS):
            add_residual(LATE, g)
            store(LATE, g, g + 1)
